import numpy as np
import ml_dtypes


def mxq(x, axis, fmt="e4m3"):
    dtype, down = {"e4m3": (ml_dtypes.float8_e4m3fn, 7), "e5m2": (ml_dtypes.float8_e5m2, 14)}[fmt]
    v = np.moveaxis(np.asarray(x, np.float32).astype(ml_dtypes.bfloat16).astype(np.float64), axis, -1)
    blocks = v.reshape(v.shape[:-1] + (-1, 32))
    amax = np.abs(blocks).max(-1, keepdims=True)
    byte = np.maximum(np.where(amax > 0, np.frexp(amax)[1] - 1 + 127, 0) - down, 1)
    scale = np.exp2(byte - 127.0)
    codes = (blocks / scale).astype(np.float32).astype(dtype).astype(np.float64)
    return np.moveaxis((codes * scale).reshape(v.shape), -1, axis)


WIDE = False


def mx_kscale(k):
    if not WIDE:
        return np.ones(k)
    levels = np.array([10, -10, 5, -5, 0])
    if k % 512:
        return np.exp2(np.random.permutation(np.resize(levels, k // 32))).repeat(32)
    a = np.empty((k // 512, 16))
    for p in range(k // 512):
        a[p, :8] = np.random.permutation(np.resize(levels, 8))
        for g in range(8):
            far = levels[np.abs(levels - a[p, g]) >= 10]
            a[p, g + 8] = far[np.random.randint(len(far))]
    return np.exp2(a.ravel()).repeat(32)


def f64(x):
    return np.asarray(x).astype(np.float64)


def striped(idx):
    return np.tile(np.asarray(idx).reshape(-1, 16).T, (8, 1)).astype(np.uint16)


def unstriped(offs):
    return offs[:16].T.reshape(-1).astype(np.int64)


def striped8(idx):
    return np.asarray(idx).reshape(8, -1, 16).transpose(0, 2, 1).reshape(128, -1).astype(np.uint16)


def unstriped8(offs):
    return offs.reshape(8, 16, -1).transpose(0, 2, 1).reshape(8, -1).astype(np.int64)


def pick8(x, idx, run):
    r = np.arange(len(x))
    return x[r[:, None], idx[r % (8 * run) // run]]


E2M1 = np.array([0.0, 0.5, 1.0, 1.5, 2.0, 3.0, 4.0, 6.0, -0.0, -0.5, -1.0, -1.5, -2.0, -3.0, -4.0, -6.0])


def pack_weight(w, fmt):
    k, n = w.shape
    w = f64(np.asarray(w, np.float32).astype(ml_dtypes.bfloat16)).reshape(k // 32, 32, n)
    amax = np.abs(w).max(1)
    if fmt == "e4m3":
        byte = np.frexp(amax)[1] - 1 + 127 - 7
    else:
        mant, ex = np.frexp(amax / 6.0)
        byte = np.where(mant > 0.5, ex, ex - 1) + 127
    byte = np.clip(np.where(amax > 0, byte, 1), 1, 254)
    scaled = (w * np.exp2(127.0 - byte)[:, None, :]).reshape(k, n).astype(np.float32)
    by_word = np.ascontiguousarray(scaled.reshape(k // 512, 128, 4, n).transpose(0, 1, 3, 2))
    if fmt == "e4m3":
        words = by_word.astype(ml_dtypes.float8_e4m3fn).view(np.uint8)
    else:
        c = by_word.astype(ml_dtypes.float4_e2m1fn).view(np.uint8) & 0xF
        words = (c[..., 0::2] | (c[..., 1::2] << 4)).reshape(k // 512, 128, 2 * n)
    return np.ascontiguousarray(words), np.ascontiguousarray(byte.astype(np.uint8).reshape(k // 512, 16, n))


def unpack_weight(words, scales, fmt):
    g, _, n = scales.shape
    words = np.ascontiguousarray(words).reshape(g, 128, n, -1)
    if fmt == "e4m3":
        vals = words.view(ml_dtypes.float8_e4m3fn).astype(np.float64)
    else:
        nib = np.empty((g, 128, n, 4), np.uint8)
        nib[..., 0::2] = words & 0xF
        nib[..., 1::2] = words >> 4
        vals = E2M1[nib]
    vals = vals * np.repeat(np.exp2(scales.astype(np.float64) - 127.0), 8, axis=1)[..., None]
    return vals.transpose(0, 1, 3, 2).reshape(g * 512, n)


K, J, R, T, F, G, I, O, N, S, Z = 512, 256, 512, 1024, 1024, 512, 256, 128, 256, 512, 1024


def setup_inputs():
    n = np.random.standard_normal
    idx = np.random.permutation(T)[:J]
    idx2 = np.stack([np.random.permutation(F)[:R] for _ in range(8)])
    idx3 = np.stack([np.random.permutation(G)[:I] for _ in range(8)])
    idx4 = np.stack([np.random.permutation(R)[:I] for _ in range(8)])
    idx5 = np.stack([np.random.permutation(J)[:O] for _ in range(8)])
    idx6 = np.random.permutation(Z)[:O]
    fk = mx_kscale(K)
    fr = mx_kscale(R)
    fs = mx_kscale(S)
    xtp = pack_weight(n((K, T)) * fk[:, None], "e4m3")
    wbp = pack_weight(n((R, N)) * 1 / np.sqrt(R) / fr[:, None], "e2m1")
    xrp = pack_weight(n((S, Z)) / fs[:, None], "e2m1")
    wsp = pack_weight(n((S, N)) * 1 / np.sqrt(S) * fs[:, None], "e4m3")
    return {
        "xt_words": xtp[0],
        "xt_scales": xtp[1],
        "ua": (np.random.randint(-7, 8, (K, F)).astype(np.float64)).astype(np.float32),
        "ub": (np.random.randint(-7, 8, (K, G)).astype(np.float64)).astype(np.float32),
        "ha": ((np.random.randint(10, 25, (K, 1)) / 1024.0) / fk[:, None]).astype(np.float32),
        "hb": ((np.random.randint(4, 13, (K, 1)) / 1024.0) / fk[:, None]).astype(np.float32),
        "sa": (np.random.uniform(0.5, 1.6, (R, 1)) * fr[:, None]).astype(np.float32),
        "wb_words": wbp[0],
        "wb_scales": wbp[1],
        "xr_words": xrp[0],
        "xr_scales": xrp[1],
        "ws_words": wsp[0],
        "ws_scales": wsp[1],
        "offs": striped(idx),
        "offs2": striped8(idx2),
        "offs3": striped8(idx3),
        "offs4": striped8(idx4),
        "offs5": striped8(idx5),
        "offs6": striped(idx6),
    }


def reference(xt_words, xt_scales, ua, ub, ha, hb, sa, wb_words, wb_scales, xr_words, xr_scales, ws_words, ws_scales, offs, offs2, offs3, offs4, offs5, offs6):
    idx = unstriped(offs)
    idx2 = unstriped8(offs2)
    idx3 = unstriped8(offs3)
    idx4 = unstriped8(offs4)
    idx5 = unstriped8(offs5)
    idx6 = unstriped(offs6)
    xtu = unpack_weight(xt_words, xt_scales, "e4m3")
    wbu = unpack_weight(wb_words, wb_scales, "e2m1")
    xru = unpack_weight(xr_words, xr_scales, "e2m1")
    wsu = unpack_weight(ws_words, ws_scales, "e4m3")
    wcd = pick8(f64(ub), idx3, 64) * f64(hb)
    wcp = np.zeros((K, R))
    wcp[np.arange(K)[:, None], idx4[np.arange(K) % 512 // 64]] = wcd
    wc = pick8(f64(ua), idx2, 64) * f64(ha) + wcp
    wcq = mxq(wc, 0, "e4m3")
    xtidxg = xtu[:, idx]
    a = wcq.T @ xtidxg
    g1 = np.maximum(a, 0.0)
    hid = pick8(g1, idx5, 64) * f64(sa)
    hidq = mxq(hid, 0, "e4m3")
    xridx6g = xru[:, idx6]
    y = wbu.T @ hidq + wsu.T @ xridx6g
    return y

@@ -1,0 +1,198 @@
+from contextlib import ExitStack
+
+import concourse.mybir as mybir
+
+K, J, R, T, F, G, I, O, N, S, Z = 512, 256, 512, 1024, 1024, 512, 256, 128, 256, 512, 1024
+FLOPS = 2 * K * R * J + 2 * R * N * O + 2 * S * N * O
+
+F32 = mybir.dt.float32
+BF16 = mybir.dt.bfloat16
+I32 = mybir.dt.int32
+U32 = mybir.dt.uint32
+U16 = mybir.dt.uint16
+U8 = mybir.dt.uint8
+FP8X4 = mybir.dt.float8_e4m3fn_x4
+FP4X4 = mybir.dt.float4_e2m1fn_x4
+COPY = mybir.ActivationFunctionType.Copy
+RELU = mybir.ActivationFunctionType.Relu
+ADD = mybir.AluOpType.add
+
+P = 128
+PACK = 4
+QUADS = 4
+HALF = R // 2
+M_HALF = HALF // PACK
+
+
+def tile_picked_tokens_refinedsome_one_kept_reminder_plain_kernel(
+    tc, xt_words, xt_scales, ua, ub, ha, hb, sa, wb_words, wb_scales, xr_words, xr_scales,
+    ws_words, ws_scales, offs, offs2, offs3, offs4, offs5, offs6, out,
+):
+    nc = tc.nc
+    with ExitStack() as ctx:
+        pool = ctx.enter_context(tc.tile_pool(name="keep", bufs=1))
+        psum = ctx.enter_context(tc.psum_pool(name="psum", bufs=1))
+
+        def load_list(source, name):
+            tile = pool.tile(list(source.shape), U16, name=name)
+            nc.sync.dma_start(tile[:], source)
+            return tile
+
+        def load_steps(source, name):
+            tile = pool.tile([P, PACK], F32, name=name)
+            nc.sync.dma_start(tile[:], source.rearrange("(p j) one -> p (j one)", j=PACK))
+            return tile
+
+        def load_rows(source, j, name):
+            tile = pool.tile([P, source.shape[1]], F32, name=name)
+            nc.sync.dma_start(tile[:], source.rearrange("(p j) c -> p j c", j=PACK)[:, j, :])
+            return tile
+
+        def load_bytes(source, name):
+            tile = pool.tile(list(source.shape), U8, name=name, tag=name, align_bytes=64)
+            nc.sync.dma_start(tile[:].bitcast(I32), source.bitcast(I32))
+            return tile
+
+        def load_scales(source, name):
+            width = source.shape[2]
+            plane = pool.tile([P, width], U8, name=name, align_bytes=64)
+            nc.vector.memset(plane[:].bitcast(I32), 0)
+            staged = pool.tile([QUADS, QUADS, width // 4], I32, name=name + "_staged")
+            nc.sync.dma_start(staged[:], source[0].bitcast(I32).rearrange("(q i) w -> i q w", i=QUADS))
+            for q in range(QUADS):
+                nc.vector.tensor_copy(plane[32 * q : 32 * q + QUADS, :].bitcast(I32), staged[:, q, :])
+            return plane
+
+        wcp = [pool.tile([P, R], F32, name="wcp%d" % j) for j in range(PACK)]
+        for j in range(PACK):
+            nc.vector.memset(wcp[j][:], 0.0)
+
+        ub_rows = [load_rows(ub, 0, "ub0")]
+        list3 = load_list(offs3, "list3")
+        hb_sb = load_steps(hb, "hb_sb")
+        ub_rows.append(load_rows(ub, 1, "ub1"))
+        ub_rows.append(load_rows(ub, 2, "ub2"))
+        list4 = load_list(offs4, "list4")
+        ub_rows.append(load_rows(ub, 3, "ub3"))
+
+        xt_plane = load_scales(xt_scales, "xt_plane")
+        xr_plane = load_scales(xr_scales, "xr_plane")
+        ws_plane = load_scales(ws_scales, "ws_plane")
+        wb_plane = load_scales(wb_scales, "wb_plane")
+        list1 = load_list(offs, "list1")
+        list6 = load_list(offs6, "list6")
+        xr_sb = load_bytes(xr_words[0], "xr_sb")
+        xt_sb = load_bytes(xt_words[0].rearrange("p c r -> p (c r)"), "xt_sb")
+        ua_rows = [load_rows(ua, j, "ua%d" % j) for j in range(PACK)]
+        ha_sb = load_steps(ha, "ha_sb")
+        list2 = load_list(offs2, "list2")
+        ws_sb = load_bytes(ws_words[0].rearrange("p c r -> p (c r)"), "ws_sb")
+        wb_sb = load_bytes(wb_words[0], "wb_sb")
+        sa_sb = load_steps(sa, "sa_sb")
+        list5 = load_list(offs5, "list5")
+
+        wcd = [pool.tile([P, I], F32, name="wcd%d" % j) for j in range(PACK)]
+        for j in range(PACK):
+            nc.scalar.activation(wcd[j][:], ub_rows[j][:].indirect(list3[:]), COPY, scale=hb_sb[:, j : j + 1])
+        for j in range(PACK):
+            nc.scalar.activation(wcp[j][:].indirect(list4[:]), wcd[j][:], COPY)
+
+        xt_codes = pool.tile([P, J], U32, name="xt_codes", align_bytes=64)
+        xt_bytes = pool.tile([P, J], U8, name="xt_bytes", align_bytes=64)
+        nc.vector.tensor_copy(xt_codes[:], xt_sb[:].bitcast(U32).indirect(list1[:]))
+        nc.vector.tensor_copy(xt_bytes[:], xt_plane[:].indirect(list1[:]))
+        xr_codes = pool.tile([P, 2 * O], U8, name="xr_codes", align_bytes=64)
+        xr_bytes = pool.tile([P, O], U8, name="xr_bytes", align_bytes=64)
+        nc.vector.tensor_copy(xr_codes[:].bitcast(U16), xr_sb[:].bitcast(U16).indirect(list6[:]))
+        nc.vector.tensor_copy(xr_bytes[:], xr_plane[:].indirect(list6[:]))
+
+        y_ps = [psum.tile([P, O], F32, name="y_ps%d" % b) for b in range(N // P)]
+        for b in range(N // P):
+            nc.tensor.matmul_mx(
+                y_ps[b][:],
+                lhsT=ws_sb[:, 4 * P * b : 4 * P * (b + 1)].bitcast(FP8X4),
+                lhsT_scale=ws_plane[:, P * b : P * (b + 1)],
+                rhs=xr_codes[:].bitcast(FP4X4),
+                rhs_scale=xr_bytes[:],
+                start=True,
+                stop=False,
+            )
+
+        detail = [
+            pool.tile([P, 2, 2, HALF], F32, name="detail0"),
+            pool.tile([P, 2, 2, HALF], F32, name="detail1", tag="xt_sb", align_bytes=64),
+        ]
+        for j in range(PACK):
+            nc.vector.tensor_copy(detail[j // 2][:, :, j % 2, :], wcp[j][:].rearrange("p (h c) -> p h c", h=2))
+
+        wc_codes = [pool.tile([P, P], U32, name="wc_codes%d" % t, align_bytes=64) for t in range(PACK)]
+        wc_bytes = [pool.tile([P, P], U8, name="wc_bytes%d" % t, align_bytes=64) for t in range(PACK)]
+        for h in range(2):
+            coarse = [pool.tile([P, 2, HALF], F32, name="coarse%d%d" % (h, u)) for u in range(2)]
+            for j in range(PACK):
+                nc.scalar.activation(
+                    coarse[j // 2][:, j % 2, :],
+                    ua_rows[j][:].indirect(list2[:, h * HALF // 16 : (h + 1) * HALF // 16]),
+                    COPY,
+                    scale=ha_sb[:, j : j + 1],
+                )
+            grouped = pool.tile([P, PACK, M_HALF, PACK], BF16, name="grouped%d" % h, align_bytes=64)
+            for u in range(2):
+                spans = [(0, 2), (2, 4)] if (h, u) == (1, 1) else [(0, 4)]
+                for t0, t1 in spans:
+                    nc.vector.tensor_tensor(
+                        grouped[:, t0:t1, :, 2 * u : 2 * u + 2].rearrange("p t m j -> p m j t"),
+                        coarse[u][:].rearrange("p j (m t) -> p m j t", t=PACK)[:, :, :, t0:t1],
+                        detail[u][:, h].rearrange("p j (m t) -> p m j t", t=PACK)[:, :, :, t0:t1],
+                        ADD,
+                    )
+            cols = slice(h * M_HALF, (h + 1) * M_HALF)
+            for t in range(PACK):
+                nc.vector.quantize_mx(
+                    wc_codes[t][:, cols].bitcast(FP8X4),
+                    wc_bytes[t][:, cols],
+                    grouped[:, t].rearrange("p m j -> p (m j)"),
+                )
+
+        hid = [pool.tile([P, 2, O], BF16, name="hid%d" % u) for u in range(2)]
+        for t in range(PACK):
+            a_ps = psum.tile([P, J], F32, name="a_ps%d" % t)
+            nc.tensor.matmul_mx(
+                a_ps[:],
+                lhsT=wc_codes[t][:].bitcast(FP8X4),
+                lhsT_scale=wc_bytes[t][:],
+                rhs=xt_codes[:].bitcast(FP8X4),
+                rhs_scale=xt_bytes[:],
+                start=True,
+                stop=True,
+            )
+            g1 = pool.tile([P, J], F32, name="g1_%d" % t)
+            if t == 0:
+                nc.scalar.activation(g1[:], a_ps[:], RELU)
+            else:
+                nc.vector.tensor_scalar_max(g1[:], a_ps[:], 0.0)
+            nc.scalar.activation(hid[t // 2][:, t % 2, :], g1[:].indirect(list5[:]), COPY, scale=sa_sb[:, t : t + 1])
+
+        hid_grouped = pool.tile([P, O, PACK], BF16, name="hid_grouped", align_bytes=64)
+        for u in range(2):
+            nc.vector.tensor_copy(hid_grouped[:, :, 2 * u : 2 * u + 2], hid[u][:].rearrange("p t o -> p o t"))
+        hid_codes = pool.tile([P, O], U32, name="hid_codes", align_bytes=64)
+        hid_bytes = pool.tile([P, O], U8, name="hid_bytes", align_bytes=64)
+        nc.vector.quantize_mx(hid_codes[:].bitcast(FP8X4), hid_bytes[:], hid_grouped[:].rearrange("p o t -> p (o t)"))
+
+        for b in range(N // P):
+            nc.tensor.matmul_mx(
+                y_ps[b][:],
+                lhsT=wb_sb[:, 2 * P * b : 2 * P * (b + 1)].bitcast(FP4X4),
+                lhsT_scale=wb_plane[:, P * b : P * (b + 1)],
+                rhs=hid_codes[:].bitcast(FP8X4),
+                rhs_scale=hid_bytes[:],
+                start=False,
+                stop=True,
+            )
+        y0 = pool.tile([P, O], F32, name="y0")
+        nc.vector.tensor_copy(y0[:], y_ps[0][:])
+        nc.sync.dma_start(out[0:P, :], y0[:])
+        y1 = pool.tile([P, O], F32, name="y1")
+        nc.scalar.copy(y1[:], y_ps[1][:])
+        nc.scalar.dma_start(out[P : 2 * P, :], y1[:])

@@ -49,7 +49,7 @@ def tile_picked_tokens_refinedsome_one_kept_reminder_plain_kernel(
             return tile
 
         def load_bytes(source, name):
-            tile = pool.tile(list(source.shape), U8, name=name, tag=name, align_bytes=64)
+            tile = pool.tile(list(source.shape), U8, name=name, align_bytes=64)
             nc.sync.dma_start(tile[:].bitcast(I32), source.bitcast(I32))
             return tile
 
@@ -118,41 +118,39 @@ def tile_picked_tokens_refinedsome_one_kept_reminder_plain_kernel(
                 stop=False,
             )
 
-        detail = [
-            pool.tile([P, 2, 2, HALF], F32, name="detail0"),
-            pool.tile([P, 2, 2, HALF], F32, name="detail1", tag="xt_sb", align_bytes=64),
-        ]
-        for j in range(PACK):
-            nc.vector.tensor_copy(detail[j // 2][:, :, j % 2, :], wcp[j][:].rearrange("p (h c) -> p h c", h=2))
-
         wc_codes = [pool.tile([P, P], U32, name="wc_codes%d" % t, align_bytes=64) for t in range(PACK)]
         wc_bytes = [pool.tile([P, P], U8, name="wc_bytes%d" % t, align_bytes=64) for t in range(PACK)]
         for h in range(2):
-            coarse = [pool.tile([P, 2, HALF], F32, name="coarse%d%d" % (h, u)) for u in range(2)]
+            dealt = pool.tile([P, PACK, PACK, M_HALF], F32, name="dealt%d" % h)
             for j in range(PACK):
+                coarse = pool.tile([P, HALF], F32, name="coarse%d%d" % (h, j))
                 nc.scalar.activation(
-                    coarse[j // 2][:, j % 2, :],
+                    coarse[:],
                     ua_rows[j][:].indirect(list2[:, h * HALF // 16 : (h + 1) * HALF // 16]),
                     COPY,
                     scale=ha_sb[:, j : j + 1],
                 )
-            grouped = pool.tile([P, PACK, M_HALF, PACK], BF16, name="grouped%d" % h, align_bytes=64)
-            for u in range(2):
-                spans = [(0, 2), (2, 4)] if (h, u) == (1, 1) else [(0, 4)]
-                for t0, t1 in spans:
-                    nc.vector.tensor_tensor(
-                        grouped[:, t0:t1, :, 2 * u : 2 * u + 2].rearrange("p t m j -> p m j t"),
-                        coarse[u][:].rearrange("p j (m t) -> p m j t", t=PACK)[:, :, :, t0:t1],
-                        detail[u][:, h].rearrange("p j (m t) -> p m j t", t=PACK)[:, :, :, t0:t1],
-                        ADD,
-                    )
-            cols = slice(h * M_HALF, (h + 1) * M_HALF)
-            for t in range(PACK):
-                nc.vector.quantize_mx(
-                    wc_codes[t][:, cols].bitcast(FP8X4),
-                    wc_bytes[t][:, cols],
-                    grouped[:, t].rearrange("p m j -> p (m j)"),
+                nc.vector.tensor_tensor(
+                    dealt[:, j].rearrange("p t m -> p m t"),
+                    coarse[:].rearrange("p (m t) -> p m t", t=PACK),
+                    wcp[j][:, h * HALF : (h + 1) * HALF].rearrange("p (m t) -> p m t", t=PACK),
+                    ADD,
                 )
+            grouped = [pool.tile([P, M_HALF, PACK], BF16, name="grouped%d%d" % (h, t), align_bytes=64) for t in range(PACK)]
+            cols = slice(h * M_HALF, (h + 1) * M_HALF)
+            for step in range(PACK + 1):
+                if step < PACK:
+                    nc.vector.tensor_copy(
+                        grouped[step][:].rearrange("p (c i) j -> p c j i", i=4),
+                        dealt[:, :, step, :].rearrange("p j (c i) -> p c j i", i=4),
+                    )
+                if step > 0:
+                    t = step - 1
+                    nc.vector.quantize_mx(
+                        wc_codes[t][:, cols].bitcast(FP8X4),
+                        wc_bytes[t][:, cols],
+                        grouped[t][:].rearrange("p m j -> p (m j)"),
+                    )
 
         hid = [pool.tile([P, 2, O], BF16, name="hid%d" % u) for u in range(2)]
         for t in range(PACK):

@@ -67,6 +67,9 @@ def tile_picked_tokens_refinedsome_one_kept_reminder_plain_kernel(
         for j in range(PACK):
             nc.vector.memset(wcp[j][:], 0.0)
 
+        warm = pool.tile([P, 2], F32, name="warm")
+        nc.vector.memset(warm[:, 0:1], 0.0)
+        nc.scalar.activation(warm[:, 1:2], warm[:, 0:1], COPY)
         ub_rows = [load_rows(ub, 0, "ub0")]
         list3 = load_list(offs3, "list3")
         hb_sb = load_steps(hb, "hb_sb")

@@ -22,6 +22,7 @@ PACK = 4
 QUADS = 4
 HALF = R // 2
 M_HALF = HALF // PACK
+EARLY = 2
 
 
 def tile_picked_tokens_refinedsome_one_kept_reminder_plain_kernel(
@@ -53,23 +54,28 @@ def tile_picked_tokens_refinedsome_one_kept_reminder_plain_kernel(
             nc.sync.dma_start(tile[:].bitcast(I32), source.bitcast(I32))
             return tile
 
-        def load_scales(source, name):
-            width = source.shape[2]
+        def zeroed_plane(width, name):
             plane = pool.tile([P, width], U8, name=name, align_bytes=64)
             nc.vector.memset(plane[:].bitcast(I32), 0)
-            staged = pool.tile([QUADS, QUADS, width // 4], I32, name=name + "_staged")
-            nc.sync.dma_start(staged[:], source[0].bitcast(I32).rearrange("(q i) w -> i q w", i=QUADS))
-            for q in range(QUADS):
-                nc.vector.tensor_copy(plane[32 * q : 32 * q + QUADS, :].bitcast(I32), staged[:, q, :])
             return plane
 
-        wcp = [pool.tile([P, R], F32, name="wcp%d" % j) for j in range(PACK)]
-        for j in range(PACK):
-            nc.vector.memset(wcp[j][:], 0.0)
+        def place_scale_rows(plane, rows):
+            for q in range(QUADS):
+                nc.sync.dma_start(plane[32 * q : 32 * q + 4, :].bitcast(I32), rows[4 * q : 4 * q + 4, :].bitcast(I32))
 
         warm = pool.tile([P, 2], F32, name="warm")
         nc.vector.memset(warm[:, 0:1], 0.0)
         nc.scalar.activation(warm[:, 1:2], warm[:, 0:1], COPY)
+        xt_rows = zeroed_plane(T, "xt_rows")
+        xr_rows = zeroed_plane(Z, "xr_rows")
+        wcp = [pool.tile([P, R], F32, name="wcp%d" % j) for j in range(PACK)]
+        for j in range(PACK):
+            nc.vector.memset(wcp[j][:], 0.0)
+        xt_plane = zeroed_plane(J, "xt_plane")
+        xr_plane = zeroed_plane(O, "xr_plane")
+        ws_plane = zeroed_plane(N, "ws_plane")
+        wb_plane = zeroed_plane(N, "wb_plane")
+
         ub_rows = [load_rows(ub, 0, "ub0")]
         list3 = load_list(offs3, "list3")
         hb_sb = load_steps(hb, "hb_sb")
@@ -78,17 +84,20 @@ def tile_picked_tokens_refinedsome_one_kept_reminder_plain_kernel(
         list4 = load_list(offs4, "list4")
         ub_rows.append(load_rows(ub, 3, "ub3"))
 
-        xt_plane = load_scales(xt_scales, "xt_plane")
-        xr_plane = load_scales(xr_scales, "xr_plane")
-        ws_plane = load_scales(ws_scales, "ws_plane")
-        wb_plane = load_scales(wb_scales, "wb_plane")
+        xt_sb = load_bytes(xt_words[0].rearrange("p c r -> p (c r)"), "xt_sb")
+        xr_sb = load_bytes(xr_words[0], "xr_sb")
+        nc.sync.dma_start(xt_rows[0:16, :].bitcast(I32), xt_scales[0].bitcast(I32))
+        nc.sync.dma_start(xr_rows[0:16, :].bitcast(I32), xr_scales[0].bitcast(I32))
         list1 = load_list(offs, "list1")
         list6 = load_list(offs6, "list6")
-        xr_sb = load_bytes(xr_words[0], "xr_sb")
-        xt_sb = load_bytes(xt_words[0].rearrange("p c r -> p (c r)"), "xt_sb")
-        ua_rows = [load_rows(ua, j, "ua%d" % j) for j in range(PACK)]
+        ua_rows = [load_rows(ua, j, "ua%d" % j) for j in range(PACK - 1)]
+        ua_last = pool.tile([P, F], F32, name="ua3")
+        ua_rows.append(ua_last)
+        ua_source = ua.rearrange("(p j) c -> p j c", j=PACK)[:, PACK - 1, :]
+        nc.sync.dma_start(ua_last[:, : F // 2], ua_source[:, : F // 2])
         ha_sb = load_steps(ha, "ha_sb")
         list2 = load_list(offs2, "list2")
+        nc.sync.dma_start(ua_last[:, F // 2 :], ua_source[:, F // 2 :])
         ws_sb = load_bytes(ws_words[0].rearrange("p c r -> p (c r)"), "ws_sb")
         wb_sb = load_bytes(wb_words[0], "wb_sb")
         sa_sb = load_steps(sa, "sa_sb")
@@ -103,11 +112,15 @@ def tile_picked_tokens_refinedsome_one_kept_reminder_plain_kernel(
         xt_codes = pool.tile([P, J], U32, name="xt_codes", align_bytes=64)
         xt_bytes = pool.tile([P, J], U8, name="xt_bytes", align_bytes=64)
         nc.vector.tensor_copy(xt_codes[:], xt_sb[:].bitcast(U32).indirect(list1[:]))
-        nc.vector.tensor_copy(xt_bytes[:], xt_plane[:].indirect(list1[:]))
+        nc.vector.tensor_copy(xt_bytes[:], xt_rows[:].indirect(list1[:]))
         xr_codes = pool.tile([P, 2 * O], U8, name="xr_codes", align_bytes=64)
         xr_bytes = pool.tile([P, O], U8, name="xr_bytes", align_bytes=64)
         nc.vector.tensor_copy(xr_codes[:].bitcast(U16), xr_sb[:].bitcast(U16).indirect(list6[:]))
-        nc.vector.tensor_copy(xr_bytes[:], xr_plane[:].indirect(list6[:]))
+        nc.vector.tensor_copy(xr_bytes[:], xr_rows[:].indirect(list6[:]))
+        place_scale_rows(xt_plane, xt_bytes)
+        place_scale_rows(xr_plane, xr_bytes)
+        place_scale_rows(ws_plane, ws_scales[0])
+        place_scale_rows(wb_plane, wb_scales[0])
 
         y_ps = [psum.tile([P, O], F32, name="y_ps%d" % b) for b in range(N // P)]
         for b in range(N // P):
@@ -116,13 +129,28 @@ def tile_picked_tokens_refinedsome_one_kept_reminder_plain_kernel(
                 lhsT=ws_sb[:, 4 * P * b : 4 * P * (b + 1)].bitcast(FP8X4),
                 lhsT_scale=ws_plane[:, P * b : P * (b + 1)],
                 rhs=xr_codes[:].bitcast(FP4X4),
-                rhs_scale=xr_bytes[:],
+                rhs_scale=xr_plane[:],
                 start=True,
                 stop=False,
             )
 
         wc_codes = [pool.tile([P, P], U32, name="wc_codes%d" % t, align_bytes=64) for t in range(PACK)]
         wc_bytes = [pool.tile([P, P], U8, name="wc_bytes%d" % t, align_bytes=64) for t in range(PACK)]
+        grouped = pool.tile([P, PACK, P, PACK], BF16, name="grouped", align_bytes=64)
+
+        def weave(copy, dealt, t0, t1, cols):
+            copy(
+                grouped[:, t0:t1, cols, :].rearrange("p t (c i) j -> p t c j i", i=4),
+                dealt[:, :, t0:t1, :].rearrange("p j t (c i) -> p t c j i", i=4),
+            )
+
+        def quantise(t, cols):
+            nc.vector.quantize_mx(
+                wc_codes[t][:, cols].bitcast(FP8X4),
+                wc_bytes[t][:, cols],
+                grouped[:, t, cols, :].rearrange("p m j -> p (m j)"),
+            )
+
         for h in range(2):
             dealt = pool.tile([P, PACK, PACK, M_HALF], F32, name="dealt%d" % h)
             for j in range(PACK):
@@ -133,29 +161,27 @@ def tile_picked_tokens_refinedsome_one_kept_reminder_plain_kernel(
                     COPY,
                     scale=ha_sb[:, j : j + 1],
                 )
-                nc.vector.tensor_tensor(
-                    dealt[:, j].rearrange("p t m -> p m t"),
-                    coarse[:].rearrange("p (m t) -> p m t", t=PACK),
-                    wcp[j][:, h * HALF : (h + 1) * HALF].rearrange("p (m t) -> p m t", t=PACK),
-                    ADD,
-                )
-            grouped = [pool.tile([P, M_HALF, PACK], BF16, name="grouped%d%d" % (h, t), align_bytes=64) for t in range(PACK)]
+                spans = [(0, 1), (1, PACK)] if (h, j) == (1, PACK - 1) else [(0, PACK)]
+                for t0, t1 in spans:
+                    nc.vector.tensor_tensor(
+                        dealt[:, j, t0:t1].rearrange("p t m -> p m t"),
+                        coarse[:].rearrange("p (m t) -> p m t", t=PACK)[:, :, t0:t1],
+                        wcp[j][:, h * HALF : (h + 1) * HALF].rearrange("p (m t) -> p m t", t=PACK)[:, :, t0:t1],
+                        ADD,
+                    )
             cols = slice(h * M_HALF, (h + 1) * M_HALF)
-            for step in range(PACK + 1):
-                if step < PACK:
-                    nc.vector.tensor_copy(
-                        grouped[step][:].rearrange("p (c i) j -> p c j i", i=4),
-                        dealt[:, :, step, :].rearrange("p j (c i) -> p c j i", i=4),
-                    )
-                if step > 0:
-                    t = step - 1
-                    nc.vector.quantize_mx(
-                        wc_codes[t][:, cols].bitcast(FP8X4),
-                        wc_bytes[t][:, cols],
-                        grouped[t][:].rearrange("p m j -> p (m j)"),
-                    )
+            if h == 0:
+                weave(nc.vector.tensor_copy, dealt, 0, PACK, cols)
+                for t in range(EARLY):
+                    quantise(t, cols)
+            else:
+                for step in range(PACK + 1):
+                    if step < PACK:
+                        weave(nc.scalar.copy if step % 2 == 1 else nc.vector.tensor_copy, dealt, step, step + 1, cols)
+                    if step > 0:
+                        quantise(step - 1, cols if step - 1 < EARLY else slice(0, P))
 
-        hid = [pool.tile([P, 2, O], BF16, name="hid%d" % u) for u in range(2)]
+        hid = pool.tile([P, PACK, O], BF16, name="hid")
         for t in range(PACK):
             a_ps = psum.tile([P, J], F32, name="a_ps%d" % t)
             nc.tensor.matmul_mx(
@@ -163,7 +189,7 @@ def tile_picked_tokens_refinedsome_one_kept_reminder_plain_kernel(
                 lhsT=wc_codes[t][:].bitcast(FP8X4),
                 lhsT_scale=wc_bytes[t][:],
                 rhs=xt_codes[:].bitcast(FP8X4),
-                rhs_scale=xt_bytes[:],
+                rhs_scale=xt_plane[:],
                 start=True,
                 stop=True,
             )
@@ -172,14 +198,29 @@ def tile_picked_tokens_refinedsome_one_kept_reminder_plain_kernel(
                 nc.scalar.activation(g1[:], a_ps[:], RELU)
             else:
                 nc.vector.tensor_scalar_max(g1[:], a_ps[:], 0.0)
-            nc.scalar.activation(hid[t // 2][:, t % 2, :], g1[:].indirect(list5[:]), COPY, scale=sa_sb[:, t : t + 1])
+            for o0, o1 in [(0, O // 2), (O // 2, O)] if t == PACK - 1 else [(0, O)]:
+                nc.scalar.activation(
+                    hid[:, t, o0:o1],
+                    g1[:].indirect(list5[:, o0 // 16 : o1 // 16]),
+                    COPY,
+                    scale=sa_sb[:, t : t + 1],
+                )
 
-        hid_grouped = pool.tile([P, O, PACK], BF16, name="hid_grouped", align_bytes=64)
-        for u in range(2):
-            nc.vector.tensor_copy(hid_grouped[:, :, 2 * u : 2 * u + 2], hid[u][:].rearrange("p t o -> p o t"))
+        hid_grouped = [pool.tile([P, O // 2, PACK], BF16, name="hid_grouped%d" % v, align_bytes=64) for v in range(2)]
         hid_codes = pool.tile([P, O], U32, name="hid_codes", align_bytes=64)
         hid_bytes = pool.tile([P, O], U8, name="hid_bytes", align_bytes=64)
-        nc.vector.quantize_mx(hid_codes[:].bitcast(FP8X4), hid_bytes[:], hid_grouped[:].rearrange("p o t -> p (o t)"))
+        places = [slice(v * O // 2, (v + 1) * O // 2) for v in range(2)]
+        for v in range(2):
+            nc.vector.tensor_copy(
+                hid_grouped[v][:].rearrange("p (c i) t -> p c t i", i=4),
+                hid[:, :, places[v]].rearrange("p t (c i) -> p c t i", i=4),
+            )
+        for v in range(2):
+            nc.vector.quantize_mx(
+                hid_codes[:, places[v]].bitcast(FP8X4),
+                hid_bytes[:, places[v]],
+                hid_grouped[v][:].rearrange("p o t -> p (o t)"),
+            )
 
         for b in range(N // P):
             nc.tensor.matmul_mx(

from contextlib import ExitStack

import concourse.mybir as mybir

K, J, R, T, F, G, I, O, N, S, Z = 512, 256, 512, 1024, 1024, 512, 256, 128, 256, 512, 1024
FLOPS = 2 * K * R * J + 2 * R * N * O + 2 * S * N * O

F32 = mybir.dt.float32
BF16 = mybir.dt.bfloat16
I32 = mybir.dt.int32
U32 = mybir.dt.uint32
U16 = mybir.dt.uint16
U8 = mybir.dt.uint8
FP8X4 = mybir.dt.float8_e4m3fn_x4
FP4X4 = mybir.dt.float4_e2m1fn_x4
COPY = mybir.ActivationFunctionType.Copy
RELU = mybir.ActivationFunctionType.Relu
ADD = mybir.AluOpType.add

P = 128
PACK = 4
QUADS = 4
HALF = R // 2
M_HALF = HALF // PACK
EARLY = 2


def tile_picked_tokens_refinedsome_one_kept_reminder_plain_kernel(
    tc, xt_words, xt_scales, ua, ub, ha, hb, sa, wb_words, wb_scales, xr_words, xr_scales,
    ws_words, ws_scales, offs, offs2, offs3, offs4, offs5, offs6, out,
):
    nc = tc.nc
    with ExitStack() as ctx:
        pool = ctx.enter_context(tc.tile_pool(name="keep", bufs=1))
        psum = ctx.enter_context(tc.psum_pool(name="psum", bufs=1))

        def load_list(source, name):
            tile = pool.tile(list(source.shape), U16, name=name)
            nc.sync.dma_start(tile[:], source)
            return tile

        def load_steps(source, name):
            tile = pool.tile([P, PACK], F32, name=name)
            nc.sync.dma_start(tile[:], source.rearrange("(p j) one -> p (j one)", j=PACK))
            return tile

        def load_rows(source, j, name):
            tile = pool.tile([P, source.shape[1]], F32, name=name)
            nc.sync.dma_start(tile[:], source.rearrange("(p j) c -> p j c", j=PACK)[:, j, :])
            return tile

        def load_bytes(source, name):
            tile = pool.tile(list(source.shape), U8, name=name, align_bytes=64)
            nc.sync.dma_start(tile[:].bitcast(I32), source.bitcast(I32))
            return tile

        def zeroed_plane(width, name):
            plane = pool.tile([P, width], U8, name=name, align_bytes=64)
            nc.vector.memset(plane[:].bitcast(I32), 0)
            return plane

        def place_scale_rows(plane, rows):
            for q in range(QUADS):
                nc.sync.dma_start(plane[32 * q : 32 * q + 4, :].bitcast(I32), rows[4 * q : 4 * q + 4, :].bitcast(I32))

        warm = pool.tile([P, 2], F32, name="warm")
        nc.vector.memset(warm[:, 0:1], 0.0)
        nc.scalar.activation(warm[:, 1:2], warm[:, 0:1], COPY)
        xt_rows = zeroed_plane(T, "xt_rows")
        xr_rows = zeroed_plane(Z, "xr_rows")
        wcp = [pool.tile([P, R], F32, name="wcp%d" % j) for j in range(PACK)]
        for j in range(PACK):
            nc.vector.memset(wcp[j][:], 0.0)
        xt_plane = zeroed_plane(J, "xt_plane")
        xr_plane = zeroed_plane(O, "xr_plane")
        ws_plane = zeroed_plane(N, "ws_plane")
        wb_plane = zeroed_plane(N, "wb_plane")

        ub_rows = [load_rows(ub, 0, "ub0")]
        list3 = load_list(offs3, "list3")
        hb_sb = load_steps(hb, "hb_sb")
        ub_rows.append(load_rows(ub, 1, "ub1"))
        ub_rows.append(load_rows(ub, 2, "ub2"))
        list4 = load_list(offs4, "list4")
        ub_rows.append(load_rows(ub, 3, "ub3"))

        xt_sb = load_bytes(xt_words[0].rearrange("p c r -> p (c r)"), "xt_sb")
        xr_sb = load_bytes(xr_words[0], "xr_sb")
        nc.sync.dma_start(xt_rows[0:16, :].bitcast(I32), xt_scales[0].bitcast(I32))
        nc.sync.dma_start(xr_rows[0:16, :].bitcast(I32), xr_scales[0].bitcast(I32))
        list1 = load_list(offs, "list1")
        list6 = load_list(offs6, "list6")
        ua_rows = [load_rows(ua, j, "ua%d" % j) for j in range(PACK - 1)]
        ua_last = pool.tile([P, F], F32, name="ua3")
        ua_rows.append(ua_last)
        ua_source = ua.rearrange("(p j) c -> p j c", j=PACK)[:, PACK - 1, :]
        nc.sync.dma_start(ua_last[:, : F // 2], ua_source[:, : F // 2])
        ha_sb = load_steps(ha, "ha_sb")
        list2 = load_list(offs2, "list2")
        nc.sync.dma_start(ua_last[:, F // 2 :], ua_source[:, F // 2 :])
        ws_sb = load_bytes(ws_words[0].rearrange("p c r -> p (c r)"), "ws_sb")
        wb_sb = load_bytes(wb_words[0], "wb_sb")
        sa_sb = load_steps(sa, "sa_sb")
        list5 = load_list(offs5, "list5")

        wcd = [pool.tile([P, I], F32, name="wcd%d" % j) for j in range(PACK)]
        for j in range(PACK):
            nc.scalar.activation(wcd[j][:], ub_rows[j][:].indirect(list3[:]), COPY, scale=hb_sb[:, j : j + 1])
        for j in range(PACK):
            nc.scalar.activation(wcp[j][:].indirect(list4[:]), wcd[j][:], COPY)

        xt_codes = pool.tile([P, J], U32, name="xt_codes", align_bytes=64)
        xt_bytes = pool.tile([P, J], U8, name="xt_bytes", align_bytes=64)
        nc.vector.tensor_copy(xt_codes[:], xt_sb[:].bitcast(U32).indirect(list1[:]))
        nc.vector.tensor_copy(xt_bytes[:], xt_rows[:].indirect(list1[:]))
        xr_codes = pool.tile([P, 2 * O], U8, name="xr_codes", align_bytes=64)
        xr_bytes = pool.tile([P, O], U8, name="xr_bytes", align_bytes=64)
        nc.vector.tensor_copy(xr_codes[:].bitcast(U16), xr_sb[:].bitcast(U16).indirect(list6[:]))
        nc.vector.tensor_copy(xr_bytes[:], xr_rows[:].indirect(list6[:]))
        place_scale_rows(xt_plane, xt_bytes)
        place_scale_rows(xr_plane, xr_bytes)
        place_scale_rows(ws_plane, ws_scales[0])
        place_scale_rows(wb_plane, wb_scales[0])

        y_ps = [psum.tile([P, O], F32, name="y_ps%d" % b) for b in range(N // P)]
        for b in range(N // P):
            nc.tensor.matmul_mx(
                y_ps[b][:],
                lhsT=ws_sb[:, 4 * P * b : 4 * P * (b + 1)].bitcast(FP8X4),
                lhsT_scale=ws_plane[:, P * b : P * (b + 1)],
                rhs=xr_codes[:].bitcast(FP4X4),
                rhs_scale=xr_plane[:],
                start=True,
                stop=False,
            )

        wc_codes = [pool.tile([P, P], U32, name="wc_codes%d" % t, align_bytes=64) for t in range(PACK)]
        wc_bytes = [pool.tile([P, P], U8, name="wc_bytes%d" % t, align_bytes=64) for t in range(PACK)]
        grouped = pool.tile([P, PACK, P, PACK], BF16, name="grouped", align_bytes=64)

        def weave(copy, dealt, t0, t1, cols):
            copy(
                grouped[:, t0:t1, cols, :].rearrange("p t (c i) j -> p t c j i", i=4),
                dealt[:, :, t0:t1, :].rearrange("p j t (c i) -> p t c j i", i=4),
            )

        def quantise(t, cols):
            nc.vector.quantize_mx(
                wc_codes[t][:, cols].bitcast(FP8X4),
                wc_bytes[t][:, cols],
                grouped[:, t, cols, :].rearrange("p m j -> p (m j)"),
            )

        for h in range(2):
            dealt = pool.tile([P, PACK, PACK, M_HALF], F32, name="dealt%d" % h)
            for j in range(PACK):
                coarse = pool.tile([P, HALF], F32, name="coarse%d%d" % (h, j))
                nc.scalar.activation(
                    coarse[:],
                    ua_rows[j][:].indirect(list2[:, h * HALF // 16 : (h + 1) * HALF // 16]),
                    COPY,
                    scale=ha_sb[:, j : j + 1],
                )
                spans = [(0, 1), (1, PACK)] if (h, j) == (1, PACK - 1) else [(0, PACK)]
                for t0, t1 in spans:
                    nc.vector.tensor_tensor(
                        dealt[:, j, t0:t1].rearrange("p t m -> p m t"),
                        coarse[:].rearrange("p (m t) -> p m t", t=PACK)[:, :, t0:t1],
                        wcp[j][:, h * HALF : (h + 1) * HALF].rearrange("p (m t) -> p m t", t=PACK)[:, :, t0:t1],
                        ADD,
                    )
            cols = slice(h * M_HALF, (h + 1) * M_HALF)
            if h == 0:
                weave(nc.vector.tensor_copy, dealt, 0, PACK, cols)
                for t in range(EARLY):
                    quantise(t, cols)
            else:
                for step in range(PACK + 1):
                    if step < PACK:
                        weave(nc.scalar.copy if step % 2 == 1 else nc.vector.tensor_copy, dealt, step, step + 1, cols)
                    if step > 0:
                        quantise(step - 1, cols if step - 1 < EARLY else slice(0, P))

        hid = pool.tile([P, PACK, O], BF16, name="hid")
        for t in range(PACK):
            a_ps = psum.tile([P, J], F32, name="a_ps%d" % t)
            nc.tensor.matmul_mx(
                a_ps[:],
                lhsT=wc_codes[t][:].bitcast(FP8X4),
                lhsT_scale=wc_bytes[t][:],
                rhs=xt_codes[:].bitcast(FP8X4),
                rhs_scale=xt_plane[:],
                start=True,
                stop=True,
            )
            g1 = pool.tile([P, J], F32, name="g1_%d" % t)
            if t == 0:
                nc.scalar.activation(g1[:], a_ps[:], RELU)
            else:
                nc.vector.tensor_scalar_max(g1[:], a_ps[:], 0.0)
            for o0, o1 in [(0, O // 2), (O // 2, O)] if t == PACK - 1 else [(0, O)]:
                nc.scalar.activation(
                    hid[:, t, o0:o1],
                    g1[:].indirect(list5[:, o0 // 16 : o1 // 16]),
                    COPY,
                    scale=sa_sb[:, t : t + 1],
                )

        hid_grouped = [pool.tile([P, O // 2, PACK], BF16, name="hid_grouped%d" % v, align_bytes=64) for v in range(2)]
        hid_codes = pool.tile([P, O], U32, name="hid_codes", align_bytes=64)
        hid_bytes = pool.tile([P, O], U8, name="hid_bytes", align_bytes=64)
        places = [slice(v * O // 2, (v + 1) * O // 2) for v in range(2)]
        for v in range(2):
            nc.vector.tensor_copy(
                hid_grouped[v][:].rearrange("p (c i) t -> p c t i", i=4),
                hid[:, :, places[v]].rearrange("p t (c i) -> p c t i", i=4),
            )
        for v in range(2):
            nc.vector.quantize_mx(
                hid_codes[:, places[v]].bitcast(FP8X4),
                hid_bytes[:, places[v]],
                hid_grouped[v][:].rearrange("p o t -> p (o t)"),
            )

        for b in range(N // P):
            nc.tensor.matmul_mx(
                y_ps[b][:],
                lhsT=wb_sb[:, 2 * P * b : 2 * P * (b + 1)].bitcast(FP4X4),
                lhsT_scale=wb_plane[:, P * b : P * (b + 1)],
                rhs=hid_codes[:].bitcast(FP8X4),
                rhs_scale=hid_bytes[:],
                start=False,
                stop=True,
            )
        y0 = pool.tile([P, O], F32, name="y0")
        nc.vector.tensor_copy(y0[:], y_ps[0][:])
        nc.sync.dma_start(out[0:P, :], y0[:])
        y1 = pool.tile([P, O], F32, name="y1")
        nc.scalar.copy(y1[:], y_ps[1][:])
        nc.scalar.dma_start(out[P : 2 * P, :], y1[:])
